import numpy as np
import ml_dtypes


def mxq(x, axis, fmt="e4m3"):
    dtype, down = {"e4m3": (ml_dtypes.float8_e4m3fn, 7), "e5m2": (ml_dtypes.float8_e5m2, 14)}[fmt]
    v = np.moveaxis(np.asarray(x, np.float32).astype(ml_dtypes.bfloat16).astype(np.float64), axis, -1)
    blocks = v.reshape(v.shape[:-1] + (-1, 32))
    amax = np.abs(blocks).max(-1, keepdims=True)
    byte = np.maximum(np.where(amax > 0, np.frexp(amax)[1] - 1 + 127, 0) - down, 1)
    scale = np.exp2(byte - 127.0)
    codes = (blocks / scale).astype(np.float32).astype(dtype).astype(np.float64)
    return np.moveaxis((codes * scale).reshape(v.shape), -1, axis)


WIDE = False


def mx_kscale(k):
    if not WIDE:
        return np.ones(k)
    levels = np.array([10, -10, 5, -5, 0])
    if k % 512:
        return np.exp2(np.random.permutation(np.resize(levels, k // 32))).repeat(32)
    a = np.empty((k // 512, 16))
    for p in range(k // 512):
        a[p, :8] = np.random.permutation(np.resize(levels, 8))
        for g in range(8):
            far = levels[np.abs(levels - a[p, g]) >= 10]
            a[p, g + 8] = far[np.random.randint(len(far))]
    return np.exp2(a.ravel()).repeat(32)


def f64(x):
    return np.asarray(x).astype(np.float64)


def striped(idx):
    return np.tile(idx.reshape(-1, 16).T, (8, 1)).astype(np.uint16)


def unstriped(offs):
    return offs[:16].T.reshape(-1).astype(np.int64)


def pack_weight(w):
    k, n = w.shape
    w = f64(np.asarray(w, np.float32).astype(ml_dtypes.bfloat16)).reshape(k // 32, 32, n)
    amax = np.abs(w).max(1)
    byte = np.clip(np.where(amax > 0, np.frexp(amax)[1] - 1 + 127 - 7, 1), 1, 254)
    scaled = (w * np.exp2(127.0 - byte)[:, None, :]).reshape(k, n).astype(np.float32)
    words = np.ascontiguousarray(scaled.reshape(k // 512, 128, 4, n).transpose(0, 1, 3, 2)).astype(ml_dtypes.float8_e4m3fn).view(np.uint8)
    return words, np.ascontiguousarray(byte.astype(np.uint8).reshape(k // 512, 16, n))


def unpack_weight(words, scales):
    g, p, n, _ = words.shape
    vals = np.ascontiguousarray(words).view(ml_dtypes.float8_e4m3fn).astype(np.float64) * np.repeat(np.exp2(scales.astype(np.float64) - 127.0), 8, axis=1)[..., None]
    return vals.transpose(0, 1, 3, 2).reshape(g * 512, n)


K, T, S, J = 1024, 1024, 512, 256


def setup_inputs():
    n = np.random.standard_normal
    s = mx_kscale(K)[:, None]
    packed_xT = pack_weight(n((K, T)) * s)
    return {
        "x_words": packed_xT[0],
        "x_scales": packed_xT[1],
        "hT": (n((K, J)) / np.sqrt(K) / s).astype(np.float32),
        "gT": (n((K, J)) / np.sqrt(K) / s).astype(np.float32),
        "offs": striped(np.random.permutation(T)[:S]),
    }


def reference(x_words, x_scales, hT, gT, offs):
    hTq = mxq(f64(hT), 0, "e4m3")
    xq = unpack_weight(x_words, x_scales)[:, unstriped(offs)]
    y = hTq.T @ xq
    gTq = mxq(f64(gT), 0, "e4m3")
    z = gTq.T @ xq
    l = 1.5 * y - (0.5 * z)
    e = np.exp(l - l.max(axis=1, keepdims=True))
    return e / e.sum(axis=1, keepdims=True)

@@ -1,0 +1,106 @@
+import concourse.mybir as mybir
+
+F32 = mybir.dt.float32
+BF16 = mybir.dt.bfloat16
+I32 = mybir.dt.int32
+U32 = mybir.dt.uint32
+U16 = mybir.dt.uint16
+U8 = mybir.dt.uint8
+FP8X4 = mybir.dt.float8_e4m3fn_x4
+ALU = mybir.AluOpType
+ACT = mybir.ActivationFunctionType
+AXIS = mybir.AxisListType
+
+K, T, S, J = 1024, 1024, 512, 256
+P = 128
+PACK = 4
+K_PASS = P * PACK
+PASSES = K // K_PASS
+TILES = J // P
+FLOPS = 2 * 2 * K * S * J
+
+
+def tile_picked_zspec_cd_p_kernel(tc, x_words, x_scales, hT, gT, offs, out):
+    nc = tc.nc
+    with (
+        tc.tile_pool(name="keep", bufs=1) as keep,
+        tc.psum_pool(name="psum", bufs=1) as psum,
+    ):
+        offsets = keep.tile([P, S // 16], U16, name="offsets")
+        table_words = [keep.tile([P, T], I32, name=f"table_words{o}", align_bytes=64) for o in range(PASSES)]
+        table_scales = keep.tile([P, T], U8, name="table_scales", align_bytes=64)
+        picked_words = [keep.tile([P, S], U32, name=f"picked_words{o}", align_bytes=64) for o in range(PASSES)]
+        picked_scales = keep.tile([P, S], U8, name="picked_scales", align_bytes=64)
+        warm_in = keep.tile([P, 8], F32, name="warm_in")
+        warm_out = keep.tile([P, 8], F32, name="warm_out")
+
+        nc.vector.memset(table_scales[:].bitcast(I32), 0)
+        nc.vector.memset(warm_in[:], 0.0)
+        nc.scalar.activation(warm_out[:], warm_in[:], ACT.Exp)
+
+        def load_words(o):
+            nc.sync.dma_start(table_words[o][:], x_words[o].rearrange("p n t -> p (n t)").bitcast(I32))
+
+        nc.sync.dma_start(offsets[:], offs)
+        load_words(0)
+        for q in range(4):
+            nc.sync.dma_start(
+                table_scales[32 * q : 32 * q + 4 * PASSES, :].bitcast(I32),
+                x_scales[:, 4 * q : 4 * q + 4, :].bitcast(I32),
+            )
+        load_words(1)
+
+        pieces = [(m, name, o) for m in range(TILES) for name in ("g", "h") for o in range(PASSES)]
+        source = {"g": gT, "h": hT}
+        raw = {}
+        for m, name, o in pieces:
+            raw[m, name, o] = keep.tile([P, PACK, P], F32, name=f"raw_{name}{m}{o}", align_bytes=64)
+            rows = source[name][o * K_PASS : (o + 1) * K_PASS, m * P : (m + 1) * P]
+            nc.sync.dma_start(raw[m, name, o][:], rows.rearrange("(p t) c -> p t c", t=PACK))
+
+        nc.vector.tensor_copy(picked_words[0][:], table_words[0][:].bitcast(U32).indirect(offsets[:]))
+        nc.vector.tensor_copy(picked_scales[:], table_scales[:].indirect(offsets[:]))
+        nc.vector.tensor_copy(picked_words[1][:], table_words[1][:].bitcast(U32).indirect(offsets[:]))
+
+        on_vector = {(1, "h", 0), (1, "h", 1)}
+        small = {}
+        for m, name, o in pieces:
+            grouped = keep.tile([P, P * PACK], BF16, name=f"grouped_{name}{m}{o}", align_bytes=64)
+            codes = keep.tile([P, P], U32, name=f"codes_{name}{m}{o}", align_bytes=64)
+            scales = keep.tile([P, P], U8, name=f"scales_{name}{m}{o}", align_bytes=64)
+            dst = grouped[:].rearrange("p (c i t) -> p c t i", i=4, t=PACK)
+            src = raw[m, name, o][:].rearrange("p t (c i) -> p c t i", i=4)
+            if (m, name, o) in on_vector:
+                nc.vector.tensor_copy(dst, src)
+            else:
+                nc.scalar.copy(dst, src)
+            nc.vector.quantize_mx(out=codes[:].bitcast(FP8X4), scales=scales[:], in_=grouped[:])
+            if o == 0:
+                acc = psum.tile([P, S], F32, name=f"acc_{name}{m}")
+            nc.tensor.matmul_mx(
+                out=acc[:],
+                lhsT=codes[:].bitcast(FP8X4),
+                lhsT_scale=scales[:],
+                rhs=picked_words[o][:].bitcast(FP8X4),
+                rhs_scale=picked_scales[4 * o : P, :],
+                start=(o == 0),
+                stop=(o == PASSES - 1),
+            )
+            if o < PASSES - 1:
+                continue
+            if name == "g":
+                small[m] = keep.tile([P, S], F32, name=f"half_small{m}", align_bytes=64)
+                nc.scalar.activation(small[m][:], acc[:], ACT.Copy, scale=0.5)
+                continue
+            negated = keep.tile([P, S], F32, name=f"negated{m}", align_bytes=64)
+            lowest = keep.tile([P, 1], F32, name=f"lowest{m}")
+            weights = keep.tile([P, S], F32, name=f"weights{m}", align_bytes=64)
+            total = keep.tile([P, 1], F32, name=f"total{m}")
+            inverse = keep.tile([P, 1], F32, name=f"inverse{m}")
+            result = keep.tile([P, S], F32, name=f"result{m}", align_bytes=64)
+            nc.vector.scalar_tensor_tensor(negated[:], acc[:], -1.5, small[m][:], ALU.mult, ALU.add)
+            nc.vector.tensor_reduce(lowest[:], negated[:], AXIS.X, ALU.min)
+            nc.scalar.activation(weights[:], negated[:], ACT.Exp, bias=lowest[:], scale=-1.0, accum_out=total[:])
+            nc.vector.reciprocal(inverse[:], total[:])
+            nc.vector.tensor_scalar(result[:], weights[:], inverse[:], None, ALU.mult)
+            nc.sync.dma_start(out[m * P : (m + 1) * P, :], result[:])

@@ -38,69 +38,125 @@ def tile_picked_zspec_cd_p_kernel(tc, x_words, x_scales, hT, gT, offs, out):
         nc.vector.memset(warm_in[:], 0.0)
         nc.scalar.activation(warm_out[:], warm_in[:], ACT.Exp)
 
+        source = {"g": gT, "h": hT}
+        raw = {}
+
         def load_words(o):
             nc.sync.dma_start(table_words[o][:], x_words[o].rearrange("p n t -> p (n t)").bitcast(I32))
 
+        def load_scales():
+            for q in range(4):
+                nc.sync.dma_start(
+                    table_scales[32 * q : 32 * q + 4 * PASSES, :].bitcast(I32),
+                    x_scales[:, 4 * q : 4 * q + 4, :].bitcast(I32),
+                )
+
+        def load_states(name, o, tiles):
+            width = P * len(tiles)
+            staged = keep.tile([P, PACK, width], F32, name=f"raw_{name}{tiles[0]}{o}", align_bytes=64)
+            rows = source[name][o * K_PASS : (o + 1) * K_PASS, tiles[0] * P : tiles[0] * P + width]
+            nc.sync.dma_start(staged[:], rows.rearrange("(p t) c -> p t c", t=PACK))
+            for i, m in enumerate(tiles):
+                raw[m, name, o] = staged[:, :, i * P : (i + 1) * P]
+
         nc.sync.dma_start(offsets[:], offs)
         load_words(0)
-        for q in range(4):
-            nc.sync.dma_start(
-                table_scales[32 * q : 32 * q + 4 * PASSES, :].bitcast(I32),
-                x_scales[:, 4 * q : 4 * q + 4, :].bitcast(I32),
-            )
+        load_scales()
+        load_states("g", 0, [0, 1])
+        load_states("h", 0, [0, 1])
         load_words(1)
+        load_states("g", 1, [0, 1])
+        load_states("h", 1, [0])
+        load_states("h", 1, [1])
 
-        pieces = [(m, name, o) for m in range(TILES) for name in ("g", "h") for o in range(PASSES)]
-        source = {"g": gT, "h": hT}
-        raw = {}
-        for m, name, o in pieces:
-            raw[m, name, o] = keep.tile([P, PACK, P], F32, name=f"raw_{name}{m}{o}", align_bytes=64)
-            rows = source[name][o * K_PASS : (o + 1) * K_PASS, m * P : (m + 1) * P]
-            nc.sync.dma_start(raw[m, name, o][:], rows.rearrange("(p t) c -> p t c", t=PACK))
+        def gather_words(o):
+            nc.vector.tensor_copy(picked_words[o][:], table_words[o][:].bitcast(U32).indirect(offsets[:]))
 
-        nc.vector.tensor_copy(picked_words[0][:], table_words[0][:].bitcast(U32).indirect(offsets[:]))
-        nc.vector.tensor_copy(picked_scales[:], table_scales[:].indirect(offsets[:]))
-        nc.vector.tensor_copy(picked_words[1][:], table_words[1][:].bitcast(U32).indirect(offsets[:]))
+        def gather_scales():
+            nc.vector.tensor_copy(picked_scales[:], table_scales[:].indirect(offsets[:]))
 
-        on_vector = {(1, "h", 0), (1, "h", 1)}
-        small = {}
-        for m, name, o in pieces:
-            grouped = keep.tile([P, P * PACK], BF16, name=f"grouped_{name}{m}{o}", align_bytes=64)
-            codes = keep.tile([P, P], U32, name=f"codes_{name}{m}{o}", align_bytes=64)
-            scales = keep.tile([P, P], U8, name=f"scales_{name}{m}{o}", align_bytes=64)
-            dst = grouped[:].rearrange("p (c i t) -> p c t i", i=4, t=PACK)
-            src = raw[m, name, o][:].rearrange("p t (c i) -> p c t i", i=4)
+        on_vector = {(1, "h", 0), (0, "g", 1), (1, "h", 1)}
+        parts = {key: 1 for key in [(0, "g"), (0, "h"), (1, "g")]}
+        parts[1, "h"] = 1
+        banks = {}
+        grouped = {}
+
+        def cast(m, name, o):
+            grouped[m, name, o] = keep.tile([P, P * PACK], BF16, name=f"grouped_{name}{m}{o}", align_bytes=64)
+            dst = grouped[m, name, o][:].rearrange("p (c i t) -> p c t i", i=4, t=PACK)
+            src = raw[m, name, o].rearrange("p t (c i) -> p c t i", i=4)
             if (m, name, o) in on_vector:
                 nc.vector.tensor_copy(dst, src)
             else:
                 nc.scalar.copy(dst, src)
-            nc.vector.quantize_mx(out=codes[:].bitcast(FP8X4), scales=scales[:], in_=grouped[:])
-            if o == 0:
-                acc = psum.tile([P, S], F32, name=f"acc_{name}{m}")
-            nc.tensor.matmul_mx(
-                out=acc[:],
-                lhsT=codes[:].bitcast(FP8X4),
-                lhsT_scale=scales[:],
-                rhs=picked_words[o][:].bitcast(FP8X4),
-                rhs_scale=picked_scales[4 * o : P, :],
-                start=(o == 0),
-                stop=(o == PASSES - 1),
-            )
-            if o < PASSES - 1:
-                continue
-            if name == "g":
-                small[m] = keep.tile([P, S], F32, name=f"half_small{m}", align_bytes=64)
-                nc.scalar.activation(small[m][:], acc[:], ACT.Copy, scale=0.5)
-                continue
-            negated = keep.tile([P, S], F32, name=f"negated{m}", align_bytes=64)
-            lowest = keep.tile([P, 1], F32, name=f"lowest{m}")
+
+        def multiply(m, name, o):
+            codes = keep.tile([P, P], U32, name=f"codes_{name}{m}{o}", align_bytes=64)
+            scales = keep.tile([P, P], U8, name=f"scales_{name}{m}{o}", align_bytes=64)
+            nc.vector.quantize_mx(out=codes[:].bitcast(FP8X4), scales=scales[:], in_=grouped[m, name, o][:])
+            width = S // parts[m, name]
+            for u in range(parts[m, name]):
+                if o == 0:
+                    banks[m, name, u] = psum.tile([P, width], F32, name=f"acc_{name}{m}{u}")
+                cols = slice(u * width, (u + 1) * width)
+                nc.tensor.matmul_mx(
+                    out=banks[m, name, u][:],
+                    lhsT=codes[:].bitcast(FP8X4),
+                    lhsT_scale=scales[:],
+                    rhs=picked_words[o][:, cols].bitcast(FP8X4),
+                    rhs_scale=picked_scales[4 * o : P, cols],
+                    start=(o == 0),
+                    stop=(o == PASSES - 1),
+                )
+
+        gather_words(0)
+        gather_scales()
+        for name in ("g", "h"):
+            for m in range(TILES):
+                cast(m, name, 0)
+        for m, name in [(0, "g"), (1, "g"), (1, "h")]:
+            multiply(m, name, 0)
+        gather_words(1)
+        multiply(0, "h", 0)
+        for name in ("g", "h"):
+            for m in range(TILES):
+                cast(m, name, 1)
+        for name in ("g", "h"):
+            for m in range(TILES):
+                multiply(m, name, 1)
+
+        small_tag = "raw_h01"
+        negated_tag = ["grouped_h11", "negated1"]
+        small, negated, lowest = {}, {}, {}
+        both_small = keep.tile([P, TILES * S], F32, name="half_small", tag=small_tag, align_bytes=64)
+        for m in range(TILES):
+            small[m] = both_small[:, m * S : (m + 1) * S]
+            nc.scalar.activation(small[m], banks[m, "g", 0][:], ACT.Copy, scale=0.5)
+        for m in range(TILES):
+            negated[m] = keep.tile([P, S], F32, name=f"negated{m}", tag=negated_tag[m], align_bytes=64)
+            width = S // parts[m, "h"]
+            for u in range(parts[m, "h"]):
+                cols = slice(u * width, (u + 1) * width)
+                nc.vector.scalar_tensor_tensor(
+                    negated[m][:, cols], banks[m, "h", u][:], -1.5, small[m][:, cols], ALU.mult, ALU.add
+                )
+        for m in range(TILES):
+            lowest[m] = keep.tile([P, 1], F32, name=f"lowest{m}")
+            nc.vector.tensor_reduce(lowest[m][:], negated[m][:], AXIS.X, ALU.min)
+        for m in range(TILES):
+            last = m == TILES - 1
             weights = keep.tile([P, S], F32, name=f"weights{m}", align_bytes=64)
             total = keep.tile([P, 1], F32, name=f"total{m}")
             inverse = keep.tile([P, 1], F32, name=f"inverse{m}")
-            result = keep.tile([P, S], F32, name=f"result{m}", align_bytes=64)
-            nc.vector.scalar_tensor_tensor(negated[:], acc[:], -1.5, small[m][:], ALU.mult, ALU.add)
-            nc.vector.tensor_reduce(lowest[:], negated[:], AXIS.X, ALU.min)
-            nc.scalar.activation(weights[:], negated[:], ACT.Exp, bias=lowest[:], scale=-1.0, accum_out=total[:])
+            nc.scalar.activation(weights[:], negated[m][:], ACT.Exp, bias=lowest[m][:], scale=-1.0, accum_out=total[:])
             nc.vector.reciprocal(inverse[:], total[:])
-            nc.vector.tensor_scalar(result[:], weights[:], inverse[:], None, ALU.mult)
-            nc.sync.dma_start(out[m * P : (m + 1) * P, :], result[:])
+            rows = slice(m * P, (m + 1) * P)
+            split = [512, 320][m]
+            if split > 0:
+                left = keep.tile([P, split], F32, name=f"left{m}", align_bytes=64)
+                nc.vector.tensor_scalar(left[:], weights[:, :split], inverse[:], None, ALU.mult)
+                nc.sync.dma_start(out[rows, :split], left[:])
+            if split < S:
+                right = keep.tile([P, S - split], F32, name=f"right{m}", align_bytes=64)
+                nc.scalar.activation(right[:], weights[:, split:], ACT.Copy, scale=inverse[:])
+                (nc.scalar if last else nc.sync).dma_start(out[rows, split:], right[:])

import concourse.mybir as mybir

F32 = mybir.dt.float32
BF16 = mybir.dt.bfloat16
I32 = mybir.dt.int32
U32 = mybir.dt.uint32
U16 = mybir.dt.uint16
U8 = mybir.dt.uint8
FP8X4 = mybir.dt.float8_e4m3fn_x4
ALU = mybir.AluOpType
ACT = mybir.ActivationFunctionType
AXIS = mybir.AxisListType

K, T, S, J = 1024, 1024, 512, 256
P = 128
PACK = 4
K_PASS = P * PACK
PASSES = K // K_PASS
TILES = J // P
FLOPS = 2 * 2 * K * S * J


def tile_picked_zspec_cd_p_kernel(tc, x_words, x_scales, hT, gT, offs, out):
    nc = tc.nc
    with (
        tc.tile_pool(name="keep", bufs=1) as keep,
        tc.psum_pool(name="psum", bufs=1) as psum,
    ):
        offsets = keep.tile([P, S // 16], U16, name="offsets")
        table_words = [keep.tile([P, T], I32, name=f"table_words{o}", align_bytes=64) for o in range(PASSES)]
        table_scales = keep.tile([P, T], U8, name="table_scales", align_bytes=64)
        picked_words = [keep.tile([P, S], U32, name=f"picked_words{o}", align_bytes=64) for o in range(PASSES)]
        picked_scales = keep.tile([P, S], U8, name="picked_scales", align_bytes=64)
        warm_in = keep.tile([P, 8], F32, name="warm_in")
        warm_out = keep.tile([P, 8], F32, name="warm_out")

        nc.vector.memset(table_scales[:].bitcast(I32), 0)
        nc.vector.memset(warm_in[:], 0.0)
        nc.scalar.activation(warm_out[:], warm_in[:], ACT.Exp)

        source = {"g": gT, "h": hT}
        raw = {}

        def load_words(o):
            nc.sync.dma_start(table_words[o][:], x_words[o].rearrange("p n t -> p (n t)").bitcast(I32))

        def load_scales():
            for q in range(4):
                nc.sync.dma_start(
                    table_scales[32 * q : 32 * q + 4 * PASSES, :].bitcast(I32),
                    x_scales[:, 4 * q : 4 * q + 4, :].bitcast(I32),
                )

        def load_states(name, o, tiles):
            width = P * len(tiles)
            staged = keep.tile([P, PACK, width], F32, name=f"raw_{name}{tiles[0]}{o}", align_bytes=64)
            rows = source[name][o * K_PASS : (o + 1) * K_PASS, tiles[0] * P : tiles[0] * P + width]
            nc.sync.dma_start(staged[:], rows.rearrange("(p t) c -> p t c", t=PACK))
            for i, m in enumerate(tiles):
                raw[m, name, o] = staged[:, :, i * P : (i + 1) * P]

        nc.sync.dma_start(offsets[:], offs)
        load_words(0)
        load_scales()
        load_states("g", 0, [0, 1])
        load_states("h", 0, [0, 1])
        load_words(1)
        load_states("g", 1, [0, 1])
        load_states("h", 1, [0])
        load_states("h", 1, [1])

        def gather_words(o):
            nc.vector.tensor_copy(picked_words[o][:], table_words[o][:].bitcast(U32).indirect(offsets[:]))

        def gather_scales():
            nc.vector.tensor_copy(picked_scales[:], table_scales[:].indirect(offsets[:]))

        on_vector = {(1, "h", 0), (0, "g", 1), (1, "h", 1)}
        parts = {key: 1 for key in [(0, "g"), (0, "h"), (1, "g")]}
        parts[1, "h"] = 1
        banks = {}
        grouped = {}

        def cast(m, name, o):
            grouped[m, name, o] = keep.tile([P, P * PACK], BF16, name=f"grouped_{name}{m}{o}", align_bytes=64)
            dst = grouped[m, name, o][:].rearrange("p (c i t) -> p c t i", i=4, t=PACK)
            src = raw[m, name, o].rearrange("p t (c i) -> p c t i", i=4)
            if (m, name, o) in on_vector:
                nc.vector.tensor_copy(dst, src)
            else:
                nc.scalar.copy(dst, src)

        def multiply(m, name, o):
            codes = keep.tile([P, P], U32, name=f"codes_{name}{m}{o}", align_bytes=64)
            scales = keep.tile([P, P], U8, name=f"scales_{name}{m}{o}", align_bytes=64)
            nc.vector.quantize_mx(out=codes[:].bitcast(FP8X4), scales=scales[:], in_=grouped[m, name, o][:])
            width = S // parts[m, name]
            for u in range(parts[m, name]):
                if o == 0:
                    banks[m, name, u] = psum.tile([P, width], F32, name=f"acc_{name}{m}{u}")
                cols = slice(u * width, (u + 1) * width)
                nc.tensor.matmul_mx(
                    out=banks[m, name, u][:],
                    lhsT=codes[:].bitcast(FP8X4),
                    lhsT_scale=scales[:],
                    rhs=picked_words[o][:, cols].bitcast(FP8X4),
                    rhs_scale=picked_scales[4 * o : P, cols],
                    start=(o == 0),
                    stop=(o == PASSES - 1),
                )

        gather_words(0)
        gather_scales()
        for name in ("g", "h"):
            for m in range(TILES):
                cast(m, name, 0)
        for m, name in [(0, "g"), (1, "g"), (1, "h")]:
            multiply(m, name, 0)
        gather_words(1)
        multiply(0, "h", 0)
        for name in ("g", "h"):
            for m in range(TILES):
                cast(m, name, 1)
        for name in ("g", "h"):
            for m in range(TILES):
                multiply(m, name, 1)

        small_tag = "raw_h01"
        negated_tag = ["grouped_h11", "negated1"]
        small, negated, lowest = {}, {}, {}
        both_small = keep.tile([P, TILES * S], F32, name="half_small", tag=small_tag, align_bytes=64)
        for m in range(TILES):
            small[m] = both_small[:, m * S : (m + 1) * S]
            nc.scalar.activation(small[m], banks[m, "g", 0][:], ACT.Copy, scale=0.5)
        for m in range(TILES):
            negated[m] = keep.tile([P, S], F32, name=f"negated{m}", tag=negated_tag[m], align_bytes=64)
            width = S // parts[m, "h"]
            for u in range(parts[m, "h"]):
                cols = slice(u * width, (u + 1) * width)
                nc.vector.scalar_tensor_tensor(
                    negated[m][:, cols], banks[m, "h", u][:], -1.5, small[m][:, cols], ALU.mult, ALU.add
                )
        for m in range(TILES):
            lowest[m] = keep.tile([P, 1], F32, name=f"lowest{m}")
            nc.vector.tensor_reduce(lowest[m][:], negated[m][:], AXIS.X, ALU.min)
        for m in range(TILES):
            last = m == TILES - 1
            weights = keep.tile([P, S], F32, name=f"weights{m}", align_bytes=64)
            total = keep.tile([P, 1], F32, name=f"total{m}")
            inverse = keep.tile([P, 1], F32, name=f"inverse{m}")
            nc.scalar.activation(weights[:], negated[m][:], ACT.Exp, bias=lowest[m][:], scale=-1.0, accum_out=total[:])
            nc.vector.reciprocal(inverse[:], total[:])
            rows = slice(m * P, (m + 1) * P)
            split = [512, 320][m]
            if split > 0:
                left = keep.tile([P, split], F32, name=f"left{m}", align_bytes=64)
                nc.vector.tensor_scalar(left[:], weights[:, :split], inverse[:], None, ALU.mult)
                nc.sync.dma_start(out[rows, :split], left[:])
            if split < S:
                right = keep.tile([P, S - split], F32, name=f"right{m}", align_bytes=64)
                nc.scalar.activation(right[:], weights[:, split:], ACT.Copy, scale=inverse[:])
                (nc.scalar if last else nc.sync).dma_start(out[rows, split:], right[:])
